import numpy as np
import ml_dtypes


def mxq(x, axis, fmt="e4m3"):
    dtype, down = {"e4m3": (ml_dtypes.float8_e4m3fn, 7), "e5m2": (ml_dtypes.float8_e5m2, 14)}[fmt]
    v = np.moveaxis(np.asarray(x, np.float32).astype(ml_dtypes.bfloat16).astype(np.float64), axis, -1)
    blocks = v.reshape(v.shape[:-1] + (-1, 32))
    amax = np.abs(blocks).max(-1, keepdims=True)
    byte = np.maximum(np.where(amax > 0, np.frexp(amax)[1] - 1 + 127, 0) - down, 1)
    scale = np.exp2(byte - 127.0)
    codes = (blocks / scale).astype(np.float32).astype(dtype).astype(np.float64)
    return np.moveaxis((codes * scale).reshape(v.shape), -1, axis)


WIDE = False


def mx_kscale(k):
    if not WIDE:
        return np.ones(k)
    levels = np.array([10, -10, 5, -5, 0])
    if k % 512:
        return np.exp2(np.random.permutation(np.resize(levels, k // 32))).repeat(32)
    a = np.empty((k // 512, 16))
    for p in range(k // 512):
        a[p, :8] = np.random.permutation(np.resize(levels, 8))
        for g in range(8):
            far = levels[np.abs(levels - a[p, g]) >= 10]
            a[p, g + 8] = far[np.random.randint(len(far))]
    return np.exp2(a.ravel()).repeat(32)


def f64(x):
    return np.asarray(x).astype(np.float64)


def striped(idx):
    return np.tile(idx.reshape(-1, 16).T, (8, 1)).astype(np.uint16)


def unstriped(offs):
    return offs[:16].T.reshape(-1).astype(np.int64)


def striped8(idx):
    return np.concatenate([x.reshape(-1, 16).T for x in idx]).astype(np.uint16)


def runs(offs, k):
    lists = np.stack([offs[16 * r : 16 * r + 16].T.reshape(-1) for r in range(8)]).astype(np.int64)
    return lists[np.arange(k) % 512 // 64]


def pack_weight(w):
    k, n = w.shape
    w = f64(np.asarray(w, np.float32).astype(ml_dtypes.bfloat16)).reshape(k // 32, 32, n)
    amax = np.abs(w).max(1)
    byte = np.clip(np.where(amax > 0, np.frexp(amax)[1] - 1 + 127 - 7, 1), 1, 254)
    scaled = (w * np.exp2(127.0 - byte)[:, None, :]).reshape(k, n).astype(np.float32)
    words = np.ascontiguousarray(scaled.reshape(k // 512, 128, 4, n).transpose(0, 1, 3, 2)).astype(ml_dtypes.float8_e4m3fn).view(np.uint8)
    return words, np.ascontiguousarray(byte.astype(np.uint8).reshape(k // 512, 16, n))


def unpack_weight(words, scales):
    g, p, n, _ = words.shape
    vals = np.ascontiguousarray(words).view(ml_dtypes.float8_e4m3fn).astype(np.float64) * np.repeat(np.exp2(scales.astype(np.float64) - 127.0), 8, axis=1)[..., None]
    return vals.transpose(0, 1, 3, 2).reshape(g * 512, n)


K, T, S, V, N, H = 512, 2048, 512, 256, 512, 512


def setup_inputs():
    n = np.random.standard_normal
    s = mx_kscale(K)[:, None]
    u = mx_kscale(H)
    packed_xT = pack_weight(n((K, T)) * s)
    perm = np.stack([np.random.permutation(S) for _ in range(8)])
    perm2 = np.stack([np.random.permutation(S) for _ in range(8)])
    return {
        "x_words": packed_xT[0],
        "x_scales": packed_xT[1],
        "w1": (n((K, H)) / np.sqrt(K) / s).astype(np.float32),
        "gn": (np.random.uniform(0.5, 1.5, (H, 1)) * u[:, None]).astype(np.float32),
        "w2": (n((H, N)) / np.sqrt(H) / u[:, None]).astype(np.float32),
        "offs": striped(np.random.permutation(T)[:S]),
        "la": striped8(perm[:, :V]),
        "lb": striped8(perm[:, V:]),
        "ma": striped8(perm2[:, :V]),
        "mb": striped8(perm2[:, V:]),
    }


def reference(x_words, x_scales, w1, gn, w2, offs, la, lb, ma, mb):
    xq = unpack_weight(x_words, x_scales)[:, unstriped(offs)]
    y = mxq(f64(w1), 0, "e4m3").T @ xq
    a = y[np.arange(H)[:, None], runs(la, H)]
    b = y[np.arange(H)[:, None], runs(lb, H)]
    pb = a * b
    pa = a + b
    d1 = np.zeros((H, S))
    d1[np.arange(H)[:, None], runs(la, H)] = pa
    d2 = d1.copy()
    d2[np.arange(H)[:, None], runs(lb, H)] = pb
    z = f64(gn) * d2
    h = mxq(f64(w2), 0, "e4m3").T @ mxq(z, 0, "e4m3")
    c = h[np.arange(N)[:, None], runs(ma, N)]
    d = h[np.arange(N)[:, None], runs(mb, N)]
    ob = c - d
    oa = np.abs(c + d)
    d3 = np.zeros((N, S))
    d3[np.arange(N)[:, None], runs(ma, N)] = oa
    out = d3.copy()
    out[np.arange(N)[:, None], runs(mb, N)] = ob
    return out

@@ -1,0 +1,201 @@
+from contextlib import ExitStack
+
+import concourse.mybir as mybir
+
+K, T, S, V, H, N = 512, 2048, 512, 256, 512, 512
+FLOPS = 2 * K * H * S + 2 * H * N * S
+
+F32 = mybir.dt.float32
+BF16 = mybir.dt.bfloat16
+I32 = mybir.dt.int32
+U32 = mybir.dt.uint32
+U16 = mybir.dt.uint16
+U8 = mybir.dt.uint8
+FP8X4 = mybir.dt.float8_e4m3fn_x4
+ADD = mybir.AluOpType.add
+MULT = mybir.AluOpType.mult
+COPY = mybir.ActivationFunctionType.Copy
+ABS = mybir.ActivationFunctionType.Abs
+
+P = 128
+PACK = 4
+HALF = S // 2
+CHUNK = 128
+
+
+def tile_picked_pairpoly_none_p_kernel(
+    tc, x_words, x_scales, w1, gn, w2, offs, la, lb, ma, mb, out
+):
+    nc = tc.nc
+    with ExitStack() as ctx:
+        sb = ctx.enter_context(tc.tile_pool(name="sb", bufs=1))
+        ps = ctx.enter_context(tc.psum_pool(name="ps", bufs=1))
+
+        def tile(name, shape, dtype):
+            return sb.tile(shape, dtype, name=name, align_bytes=64)
+
+        def bank(index, width):
+            return ps.tile([P, width], F32, name="bank%d" % index)
+
+        def load_list(name, src):
+            held = sb.tile(list(src.shape), U16, name=name)
+            nc.sync.dma_start(held[:], src)
+            return held
+
+        def mx(dst, w_codes, w_scales, t, codes, scales):
+            cols = slice(t * P, (t + 1) * P)
+            nc.tensor.matmul_mx(
+                out=dst,
+                lhsT=w_codes[:, cols].bitcast(FP8X4),
+                lhsT_scale=w_scales[:, cols],
+                rhs=codes.bitcast(FP8X4),
+                rhs_scale=scales,
+                start=True,
+                stop=True,
+            )
+
+        def deal(engine_copy, grouped, raw, t):
+            engine_copy(out=grouped[:], in_=raw[:].rearrange("p j (m t) -> p t m j", t=PACK)[:, t])
+
+        def quantize_block(codes, scales, grouped, t):
+            cols = slice(t * P, (t + 1) * P)
+            nc.vector.quantize_mx(
+                out=codes[:, cols].bitcast(FP8X4),
+                scales=scales[:, cols],
+                in_=grouped[:].rearrange("p m j -> p (m j)"),
+            )
+
+        xs = tile("xs", [P, T], U8)
+        nc.vector.memset(xs[:].bitcast(I32), 0)
+        w1_raw = tile("w1_raw", [P, PACK, H], F32)
+        nc.sync.dma_start(w1_raw[:], w1.rearrange("(p j) c -> p j c", j=PACK))
+        for q in range(4):
+            nc.scalar.dma_start(
+                xs[32 * q : 32 * q + 4, :].bitcast(I32),
+                x_scales[0, 4 * q : 4 * q + 4, :].bitcast(I32),
+            )
+        offs_t = load_list("offs_t", offs)
+        xw = tile("xw", [P, T], U32)
+        nc.sync.dma_start(xw[:].bitcast(I32), x_words[0].rearrange("p n r -> p (n r)").bitcast(I32))
+        la_t = load_list("la_t", la)
+        lb_t = load_list("lb_t", lb)
+        gain = tile("gain", [P, PACK], F32)
+        nc.sync.dma_start(gain[:], gn.rearrange("(p t) o -> p (t o)", t=PACK))
+        w2_raw = tile("w2_raw", [P, PACK, N], F32)
+        nc.sync.dma_start(w2_raw[:], w2.rearrange("(p j) c -> p j c", j=PACK))
+        ma_t = load_list("ma_t", ma)
+        mb_t = load_list("mb_t", mb)
+
+        sums = [tile("sums%d" % t, [P, S], F32) for t in range(PACK)]
+        for t in range(PACK):
+            nc.vector.memset(sums[t][:], 0.0)
+
+        sg = tile("sg", [P, S], U8)
+        nc.vector.tensor_copy(sg[:], xs[:].indirect(offs_t[:]))
+
+        order = (1, 2, 3, 0)
+        lead = order[0]
+        w1_bf = [tile("w1_bf%d" % t, [P, P, PACK], BF16) for t in range(PACK)]
+        w1_codes = tile("w1_codes", [P, H], U32)
+        w1_scales = tile("w1_scales", [P, H], U8)
+        for i, t in enumerate(order):
+            deal(nc.vector.tensor_copy if i % 2 == 0 else nc.scalar.copy, w1_bf[t], w1_raw, t)
+        for t in order:
+            quantize_block(w1_codes, w1_scales, w1_bf[t], t)
+
+        xg = tile("xg", [P, S], U32)
+        y = [tile("y%d" % t, [P, S], F32) for t in range(PACK)]
+        for u in range(2):
+            cols = slice(u * HALF, (u + 1) * HALF)
+            nc.vector.tensor_copy(xg[:, cols], xw[:].indirect(offs_t[:, u * 16 : (u + 1) * 16]))
+        pieces = ((0, HALF, nc.scalar.copy), (HALF, CHUNK, nc.scalar.copy), (HALF + CHUNK, CHUNK, nc.vector.tensor_copy))
+        for i, (start, width, evacuate) in enumerate(pieces):
+            cols = slice(start, start + width)
+            acc = bank(i, width)
+            mx(acc[:], w1_codes, w1_scales, lead, xg[:, cols], sg[:, cols])
+            evacuate(y[lead][:, cols], acc[:])
+        for i, t in enumerate(order[1:]):
+            acc = bank(3 + i, S)
+            mx(acc[:], w1_codes, w1_scales, t, xg[:], sg[:])
+            nc.scalar.copy(y[t][:], acc[:])
+
+        def fetch(dst, window, lst):
+            nc.vector.tensor_copy(dst, window[:].indirect(lst[:]))
+
+        a = [tile("a%d" % t, [P, V], F32) for t in range(PACK)]
+        b = [tile("b%d" % t, [P, V], F32) for t in range(PACK)]
+        ga = [tile("ga%d" % t, [P, V], F32) for t in range(PACK)]
+        gb = [tile("gb%d" % t, [P, V], F32) for t in range(PACK)]
+        z = [tile("z%d" % t, [P, 2 * S if t == 0 else S], F32) for t in range(PACK)]
+        for t in order:
+            fetch(a[t][:], y[t], la_t)
+            fetch(b[t][:], y[t], lb_t)
+        for pair in (order[:2], order[2:]):
+            for t in pair:
+                nc.scalar.activation(ga[t][:], a[t][:], COPY, scale=gain[:, t : t + 1])
+            if 0 in pair:
+                nc.scalar.copy(z[0][:, S:], z[1][:])
+            for t in pair:
+                nc.vector.tensor_tensor(z[t][:].indirect(lb_t[:]), ga[t][:], b[t][:], MULT)
+            for t in pair:
+                nc.scalar.activation(gb[t][:], b[t][:], COPY, scale=gain[:, t : t + 1])
+            for t in pair:
+                nc.vector.tensor_tensor(z[t][:].indirect(la_t[:]), ga[t][:], gb[t][:], ADD)
+
+        w2_bf = [tile("w2_bf%d" % t, [P, P, PACK], BF16) for t in range(PACK)]
+        for t in range(PACK):
+            deal(nc.scalar.copy, w2_bf[t], w2_raw, t)
+        w2_codes = tile("w2_codes", [P, N], U32)
+        w2_scales = tile("w2_scales", [P, N], U8)
+
+        quantize_block(w2_codes, w2_scales, w2_bf[0], 0)
+
+        chunks = S // CHUNK
+        zb = [tile("zb%d" % c, [P, CHUNK, PACK], BF16) for c in range(chunks)]
+        for t in (2, 3):
+            for c in range(chunks):
+                nc.scalar.copy(zb[c][:, :, t], z[t][:, c * CHUNK : (c + 1) * CHUNK])
+        low = z[0][:].rearrange("p (t n) -> p n t", t=2)
+        for c in range(chunks):
+            cast = nc.vector.tensor_copy if c < 2 else nc.scalar.copy
+            cast(zb[c][:, :, 0:2], low[:, c * CHUNK : (c + 1) * CHUNK])
+
+        z_codes = tile("z_codes", [P, S], U32)
+        z_scales = tile("z_scales", [P, S], U8)
+        h = [tile("h%d" % t, [P, S], F32) for t in range(PACK)]
+        for c in range(chunks):
+            cols = slice(c * CHUNK, (c + 1) * CHUNK)
+            nc.vector.quantize_mx(
+                out=z_codes[:, cols].bitcast(FP8X4),
+                scales=z_scales[:, cols],
+                in_=zb[c][:].rearrange("p n t -> p (n t)"),
+            )
+            acc = bank((6 + c) % 8, CHUNK)
+            mx(acc[:], w2_codes, w2_scales, 0, z_codes[:, cols], z_scales[:, cols])
+            evacuate = nc.scalar.copy if c + 1 < chunks else nc.vector.tensor_copy
+            evacuate(h[0][:, cols], acc[:])
+        for t in range(1, PACK):
+            quantize_block(w2_codes, w2_scales, w2_bf[t], t)
+            acc = bank(1 + t, S)
+            mx(acc[:], w2_codes, w2_scales, t, z_codes[:], z_scales[:])
+            nc.scalar.copy(h[t][:], acc[:])
+
+        cd = [tile("cd%d" % t, [P, 2 * V], F32) for t in range(PACK)]
+        neg = [tile("neg%d" % t, [P, 2 * V], F32) for t in range(PACK)]
+        res = [tile("res%d" % t, [P, S], F32) for t in range(PACK)]
+        out_rows = out.rearrange("(p t) n -> t p n", t=PACK)
+        for t in range(PACK):
+            fetch(cd[t][:, :V], h[t], ma_t)
+            fetch(cd[t][:, V:], h[t], mb_t)
+
+        def finish(t):
+            nc.scalar.activation(res[t][:], sums[t][:], ABS)
+            nc.vector.tensor_tensor(res[t][:].indirect(mb_t[:]), cd[t][:, :V], neg[t][:, V:], ADD)
+            nc.sync.dma_start(out_rows[t], res[t][:])
+
+        for t in range(PACK):
+            nc.scalar.activation(neg[t][:], cd[t][:], COPY, scale=-1.0)
+            nc.vector.tensor_tensor(sums[t][:].indirect(ma_t[:]), neg[t][:, :V], neg[t][:, V:], ADD)
+            if t > 0:
+                finish(t - 1)
+        finish(PACK - 1)

@@ -31,8 +31,8 @@ def tile_picked_pairpoly_none_p_kernel(
         sb = ctx.enter_context(tc.tile_pool(name="sb", bufs=1))
         ps = ctx.enter_context(tc.psum_pool(name="ps", bufs=1))
 
-        def tile(name, shape, dtype):
-            return sb.tile(shape, dtype, name=name, align_bytes=64)
+        def tile(name, shape, dtype, tag=None):
+            return sb.tile(shape, dtype, name=name, tag=tag or name, align_bytes=64)
 
         def bank(index, width):
             return ps.tile([P, width], F32, name="bank%d" % index)
@@ -42,12 +42,11 @@ def tile_picked_pairpoly_none_p_kernel(
             nc.sync.dma_start(held[:], src)
             return held
 
-        def mx(dst, w_codes, w_scales, t, codes, scales):
-            cols = slice(t * P, (t + 1) * P)
+        def mx(dst, w_codes, w_scales, codes, scales):
             nc.tensor.matmul_mx(
                 out=dst,
-                lhsT=w_codes[:, cols].bitcast(FP8X4),
-                lhsT_scale=w_scales[:, cols],
+                lhsT=w_codes.bitcast(FP8X4),
+                lhsT_scale=w_scales,
                 rhs=codes.bitcast(FP8X4),
                 rhs_scale=scales,
                 start=True,
@@ -55,26 +54,22 @@ def tile_picked_pairpoly_none_p_kernel(
             )
 
         def deal(engine_copy, grouped, raw, t):
-            engine_copy(out=grouped[:], in_=raw[:].rearrange("p j (m t) -> p t m j", t=PACK)[:, t])
-
-        def quantize_block(codes, scales, grouped, t):
-            cols = slice(t * P, (t + 1) * P)
-            nc.vector.quantize_mx(
-                out=codes[:, cols].bitcast(FP8X4),
-                scales=scales[:, cols],
-                in_=grouped[:].rearrange("p m j -> p (m j)"),
+            engine_copy(
+                out=grouped.rearrange("p (m j) -> p m j", j=PACK),
+                in_=raw[:].rearrange("p j (m t) -> p t m j", t=PACK)[:, t],
             )
+
+        def quantize(codes, scales, grouped):
+            nc.vector.quantize_mx(out=codes.bitcast(FP8X4), scales=scales, in_=grouped)
 
         xs = tile("xs", [P, T], U8)
-        nc.vector.memset(xs[:].bitcast(I32), 0)
+        nc.gpsimd.memset(xs[:, : T // 2].bitcast(I32), 0)
+        nc.vector.memset(xs[:, T // 2 :].bitcast(I32), 0)
         w1_raw = tile("w1_raw", [P, PACK, H], F32)
         nc.sync.dma_start(w1_raw[:], w1.rearrange("(p j) c -> p j c", j=PACK))
-        for q in range(4):
-            nc.scalar.dma_start(
-                xs[32 * q : 32 * q + 4, :].bitcast(I32),
-                x_scales[0, 4 * q : 4 * q + 4, :].bitcast(I32),
-            )
         offs_t = load_list("offs_t", offs)
+        for r in range(4):
+            nc.sync.dma_start(xs[r:P:32, :].bitcast(I32), x_scales[0, r:16:4, :].bitcast(I32))
         xw = tile("xw", [P, T], U32)
         nc.sync.dma_start(xw[:].bitcast(I32), x_words[0].rearrange("p n r -> p (n r)").bitcast(I32))
         la_t = load_list("la_t", la)
@@ -95,28 +90,37 @@ def tile_picked_pairpoly_none_p_kernel(
 
         order = (1, 2, 3, 0)
         lead = order[0]
-        w1_bf = [tile("w1_bf%d" % t, [P, P, PACK], BF16) for t in range(PACK)]
-        w1_codes = tile("w1_codes", [P, H], U32)
-        w1_scales = tile("w1_scales", [P, H], U8)
-        for i, t in enumerate(order):
-            deal(nc.vector.tensor_copy if i % 2 == 0 else nc.scalar.copy, w1_bf[t], w1_raw, t)
-        for t in order:
-            quantize_block(w1_codes, w1_scales, w1_bf[t], t)
+        width = P * PACK
+        lead_bf = tile("lead_bf", [P, width], BF16)
+        next_bf = tile("next_bf", [P, width], BF16)
+        rest_bf = tile("rest_bf", [P, 2 * width], BF16)
+        deal(nc.vector.tensor_copy, lead_bf[:], w1_raw, order[0])
+        deal(nc.scalar.copy, next_bf[:], w1_raw, order[1])
+        deal(nc.scalar.copy, rest_bf[:, :width], w1_raw, order[2])
+        deal(nc.scalar.copy, rest_bf[:, width:], w1_raw, order[3])
+        lead_codes = tile("lead_codes", [P, P], U32)
+        lead_scales = tile("lead_scales", [P, P], U8)
+        quantize(lead_codes[:], lead_scales[:], lead_bf[:])
 
-        xg = tile("xg", [P, S], U32)
+        xg = tile("xg", [P, S], U32, "xs")
         y = [tile("y%d" % t, [P, S], F32) for t in range(PACK)]
         for u in range(2):
             cols = slice(u * HALF, (u + 1) * HALF)
             nc.vector.tensor_copy(xg[:, cols], xw[:].indirect(offs_t[:, u * 16 : (u + 1) * 16]))
+        late_codes = tile("late_codes", [P, 3 * P], U32, "xw")
+        late_scales = tile("late_scales", [P, 3 * P], U8)
+        quantize(late_codes[:, :P], late_scales[:, :P], next_bf[:])
         pieces = ((0, HALF, nc.scalar.copy), (HALF, CHUNK, nc.scalar.copy), (HALF + CHUNK, CHUNK, nc.vector.tensor_copy))
-        for i, (start, width, evacuate) in enumerate(pieces):
-            cols = slice(start, start + width)
-            acc = bank(i, width)
-            mx(acc[:], w1_codes, w1_scales, lead, xg[:, cols], sg[:, cols])
+        for i, (start, span, evacuate) in enumerate(pieces):
+            cols = slice(start, start + span)
+            acc = bank(i, span)
+            mx(acc[:], lead_codes[:], lead_scales[:], xg[:, cols], sg[:, cols])
             evacuate(y[lead][:, cols], acc[:])
+        quantize(late_codes[:, P:], late_scales[:, P:], rest_bf[:])
         for i, t in enumerate(order[1:]):
+            cols = slice(i * P, (i + 1) * P)
             acc = bank(3 + i, S)
-            mx(acc[:], w1_codes, w1_scales, t, xg[:], sg[:])
+            mx(acc[:], late_codes[:, cols], late_scales[:, cols], xg[:], sg[:])
             nc.scalar.copy(y[t][:], acc[:])
 
         def fetch(dst, window, lst):
@@ -124,31 +128,50 @@ def tile_picked_pairpoly_none_p_kernel(
 
         a = [tile("a%d" % t, [P, V], F32) for t in range(PACK)]
         b = [tile("b%d" % t, [P, V], F32) for t in range(PACK)]
-        ga = [tile("ga%d" % t, [P, V], F32) for t in range(PACK)]
-        gb = [tile("gb%d" % t, [P, V], F32) for t in range(PACK)]
         z = [tile("z%d" % t, [P, 2 * S if t == 0 else S], F32) for t in range(PACK)]
         for t in order:
             fetch(a[t][:], y[t], la_t)
             fetch(b[t][:], y[t], lb_t)
-        for pair in (order[:2], order[2:]):
-            for t in pair:
-                nc.scalar.activation(ga[t][:], a[t][:], COPY, scale=gain[:, t : t + 1])
-            if 0 in pair:
-                nc.scalar.copy(z[0][:, S:], z[1][:])
-            for t in pair:
-                nc.vector.tensor_tensor(z[t][:].indirect(lb_t[:]), ga[t][:], b[t][:], MULT)
-            for t in pair:
-                nc.scalar.activation(gb[t][:], b[t][:], COPY, scale=gain[:, t : t + 1])
-            for t in pair:
-                nc.vector.tensor_tensor(z[t][:].indirect(la_t[:]), ga[t][:], gb[t][:], ADD)
+        last = order[-1]
 
-        w2_bf = [tile("w2_bf%d" % t, [P, P, PACK], BF16) for t in range(PACK)]
-        for t in range(PACK):
-            deal(nc.scalar.copy, w2_bf[t], w2_raw, t)
-        w2_codes = tile("w2_codes", [P, N], U32)
-        w2_scales = tile("w2_scales", [P, N], U8)
+        def gained(dst, src, t):
+            nc.scalar.activation(dst, src[t][:], COPY, scale=gain[:, t : t + 1])
 
-        quantize_block(w2_codes, w2_scales, w2_bf[0], 0)
+        def place(t, lst, left, right, op):
+            nc.vector.tensor_tensor(z[t][:].indirect(lst[:]), left, right, op)
+
+        early = tile("early", [P, 3, V], F32, "y%d" % order[2])
+        ga = {t: early[:, i] for i, t in enumerate(order[:-1])}
+        for t in order[:-1]:
+            gained(ga[t], a, t)
+        for t in order[:-1]:
+            place(t, lb_t, ga[t], b[t][:], MULT)
+
+        w2_bf = tile("w2_bf", [P, PACK, width], BF16)
+        for t in range(0, PACK, 2):
+            nc.scalar.copy(
+                w2_bf[:, t : t + 2].rearrange("p t (m j) -> p m t j", j=PACK),
+                w2_raw[:].rearrange("p j (m t) -> p m t j", t=PACK)[:, :, t : t + 2],
+            )
+
+        middle = tile("middle", [P, 3, V], F32, "w2_raw")
+        ga[last] = middle[:, 2]
+        for i, t in enumerate(order[:2]):
+            gained(middle[:, i], b, t)
+        gained(ga[last], a, last)
+        for i, t in enumerate(order[:2]):
+            place(t, la_t, ga[t], middle[:, i], ADD)
+        nc.scalar.copy(z[0][:, S:], z[1][:])
+        place(last, lb_t, ga[last], b[last][:], MULT)
+        late = tile("late", [P, 2, V], F32, "z1")
+        for i, t in enumerate(order[2:]):
+            gained(late[:, i], b, t)
+        for i, t in enumerate(order[2:]):
+            place(t, la_t, ga[t], late[:, i], ADD)
+
+        w2_lead_codes = tile("w2_lead_codes", [P, P], U32, "b%d" % order[2])
+        w2_lead_scales = tile("w2_lead_scales", [P, P], U8)
+        quantize(w2_lead_codes[:], w2_lead_scales[:], w2_bf[:, 0])
 
         chunks = S // CHUNK
         zb = [tile("zb%d" % c, [P, CHUNK, PACK], BF16) for c in range(chunks)]
@@ -165,19 +188,17 @@ def tile_picked_pairpoly_none_p_kernel(
         h = [tile("h%d" % t, [P, S], F32) for t in range(PACK)]
         for c in range(chunks):
             cols = slice(c * CHUNK, (c + 1) * CHUNK)
-            nc.vector.quantize_mx(
-                out=z_codes[:, cols].bitcast(FP8X4),
-                scales=z_scales[:, cols],
-                in_=zb[c][:].rearrange("p n t -> p (n t)"),
-            )
+            quantize(z_codes[:, cols], z_scales[:, cols], zb[c][:].rearrange("p n t -> p (n t)"))
             acc = bank((6 + c) % 8, CHUNK)
-            mx(acc[:], w2_codes, w2_scales, 0, z_codes[:, cols], z_scales[:, cols])
-            evacuate = nc.scalar.copy if c + 1 < chunks else nc.vector.tensor_copy
-            evacuate(h[0][:, cols], acc[:])
+            mx(acc[:], w2_lead_codes[:], w2_lead_scales[:], z_codes[:, cols], z_scales[:, cols])
+            nc.scalar.copy(h[0][:, cols], acc[:])
+        w2_late_codes = tile("w2_late_codes", [P, 3 * P], U32, "zb2")
+        w2_late_scales = tile("w2_late_scales", [P, 3 * P], U8)
         for t in range(1, PACK):
-            quantize_block(w2_codes, w2_scales, w2_bf[t], t)
+            cols = slice((t - 1) * P, t * P)
+            quantize(w2_late_codes[:, cols], w2_late_scales[:, cols], w2_bf[:, t])
             acc = bank(1 + t, S)
-            mx(acc[:], w2_codes, w2_scales, t, z_codes[:], z_scales[:])
+            mx(acc[:], w2_late_codes[:, cols], w2_late_scales[:, cols], z_codes[:], z_scales[:])
             nc.scalar.copy(h[t][:], acc[:])
 
         cd = [tile("cd%d" % t, [P, 2 * V], F32) for t in range(PACK)]

@@ -53,10 +53,10 @@ def tile_picked_pairpoly_none_p_kernel(
                 stop=True,
             )
 
-        def deal(engine_copy, grouped, raw, t):
+        def deal(engine_copy, grouped, raw, first):
             engine_copy(
-                out=grouped.rearrange("p (m j) -> p m j", j=PACK),
-                in_=raw[:].rearrange("p j (m t) -> p t m j", t=PACK)[:, t],
+                out=grouped.rearrange("p t (m j) -> p m t j", j=PACK),
+                in_=raw[:].rearrange("p j (m t) -> p m t j", t=PACK)[:, :, first : first + grouped.shape[1]],
             )
 
         def quantize(codes, scales, grouped):
@@ -91,16 +91,15 @@ def tile_picked_pairpoly_none_p_kernel(
         order = (1, 2, 3, 0)
         lead = order[0]
         width = P * PACK
-        lead_bf = tile("lead_bf", [P, width], BF16)
-        next_bf = tile("next_bf", [P, width], BF16)
-        rest_bf = tile("rest_bf", [P, 2 * width], BF16)
-        deal(nc.vector.tensor_copy, lead_bf[:], w1_raw, order[0])
-        deal(nc.scalar.copy, next_bf[:], w1_raw, order[1])
-        deal(nc.scalar.copy, rest_bf[:, :width], w1_raw, order[2])
-        deal(nc.scalar.copy, rest_bf[:, width:], w1_raw, order[3])
+        w1_bf = {}
+        for first, count, engine_copy in ((1, 1, nc.vector.tensor_copy), (2, 2, nc.scalar.copy), (0, 1, nc.scalar.copy)):
+            grouped = tile("w1_bf%d" % first, [P, count, width], BF16)
+            deal(engine_copy, grouped[:], w1_raw, first)
+            for i in range(count):
+                w1_bf[first + i] = grouped[:, i]
         lead_codes = tile("lead_codes", [P, P], U32)
         lead_scales = tile("lead_scales", [P, P], U8)
-        quantize(lead_codes[:], lead_scales[:], lead_bf[:])
+        quantize(lead_codes[:], lead_scales[:], w1_bf[lead])
 
         xg = tile("xg", [P, S], U32, "xs")
         y = [tile("y%d" % t, [P, S], F32) for t in range(PACK)]
@@ -109,14 +108,13 @@ def tile_picked_pairpoly_none_p_kernel(
             nc.vector.tensor_copy(xg[:, cols], xw[:].indirect(offs_t[:, u * 16 : (u + 1) * 16]))
         late_codes = tile("late_codes", [P, 3 * P], U32, "xw")
         late_scales = tile("late_scales", [P, 3 * P], U8)
-        quantize(late_codes[:, :P], late_scales[:, :P], next_bf[:])
-        pieces = ((0, HALF, nc.scalar.copy), (HALF, CHUNK, nc.scalar.copy), (HALF + CHUNK, CHUNK, nc.vector.tensor_copy))
-        for i, (start, span, evacuate) in enumerate(pieces):
+        for i, t in enumerate(order[1:]):
+            quantize(late_codes[:, i * P : (i + 1) * P], late_scales[:, i * P : (i + 1) * P], w1_bf[t])
+        for i, (start, span) in enumerate(((0, HALF), (HALF, CHUNK), (HALF + CHUNK, CHUNK))):
             cols = slice(start, start + span)
             acc = bank(i, span)
             mx(acc[:], lead_codes[:], lead_scales[:], xg[:, cols], sg[:, cols])
-            evacuate(y[lead][:, cols], acc[:])
-        quantize(late_codes[:, P:], late_scales[:, P:], rest_bf[:])
+            nc.scalar.copy(y[lead][:, cols], acc[:])
         for i, t in enumerate(order[1:]):
             cols = slice(i * P, (i + 1) * P)
             acc = bank(3 + i, S)
@@ -149,10 +147,7 @@ def tile_picked_pairpoly_none_p_kernel(
 
         w2_bf = tile("w2_bf", [P, PACK, width], BF16)
         for t in range(0, PACK, 2):
-            nc.scalar.copy(
-                w2_bf[:, t : t + 2].rearrange("p t (m j) -> p m t j", j=PACK),
-                w2_raw[:].rearrange("p j (m t) -> p m t j", t=PACK)[:, :, t : t + 2],
-            )
+            deal(nc.scalar.copy, w2_bf[:, t : t + 2], w2_raw, t)
 
         middle = tile("middle", [P, 3, V], F32, "w2_raw")
         ga[last] = middle[:, 2]

from contextlib import ExitStack

import concourse.mybir as mybir

K, T, S, V, H, N = 512, 2048, 512, 256, 512, 512
FLOPS = 2 * K * H * S + 2 * H * N * S

F32 = mybir.dt.float32
BF16 = mybir.dt.bfloat16
I32 = mybir.dt.int32
U32 = mybir.dt.uint32
U16 = mybir.dt.uint16
U8 = mybir.dt.uint8
FP8X4 = mybir.dt.float8_e4m3fn_x4
ADD = mybir.AluOpType.add
MULT = mybir.AluOpType.mult
COPY = mybir.ActivationFunctionType.Copy
ABS = mybir.ActivationFunctionType.Abs

P = 128
PACK = 4
HALF = S // 2
CHUNK = 128


def tile_picked_pairpoly_none_p_kernel(
    tc, x_words, x_scales, w1, gn, w2, offs, la, lb, ma, mb, out
):
    nc = tc.nc
    with ExitStack() as ctx:
        sb = ctx.enter_context(tc.tile_pool(name="sb", bufs=1))
        ps = ctx.enter_context(tc.psum_pool(name="ps", bufs=1))

        def tile(name, shape, dtype, tag=None):
            return sb.tile(shape, dtype, name=name, tag=tag or name, align_bytes=64)

        def bank(index, width):
            return ps.tile([P, width], F32, name="bank%d" % index)

        def load_list(name, src):
            held = sb.tile(list(src.shape), U16, name=name)
            nc.sync.dma_start(held[:], src)
            return held

        def mx(dst, w_codes, w_scales, codes, scales):
            nc.tensor.matmul_mx(
                out=dst,
                lhsT=w_codes.bitcast(FP8X4),
                lhsT_scale=w_scales,
                rhs=codes.bitcast(FP8X4),
                rhs_scale=scales,
                start=True,
                stop=True,
            )

        def deal(engine_copy, grouped, raw, first):
            engine_copy(
                out=grouped.rearrange("p t (m j) -> p m t j", j=PACK),
                in_=raw[:].rearrange("p j (m t) -> p m t j", t=PACK)[:, :, first : first + grouped.shape[1]],
            )

        def quantize(codes, scales, grouped):
            nc.vector.quantize_mx(out=codes.bitcast(FP8X4), scales=scales, in_=grouped)

        xs = tile("xs", [P, T], U8)
        nc.gpsimd.memset(xs[:, : T // 2].bitcast(I32), 0)
        nc.vector.memset(xs[:, T // 2 :].bitcast(I32), 0)
        w1_raw = tile("w1_raw", [P, PACK, H], F32)
        nc.sync.dma_start(w1_raw[:], w1.rearrange("(p j) c -> p j c", j=PACK))
        offs_t = load_list("offs_t", offs)
        for r in range(4):
            nc.sync.dma_start(xs[r:P:32, :].bitcast(I32), x_scales[0, r:16:4, :].bitcast(I32))
        xw = tile("xw", [P, T], U32)
        nc.sync.dma_start(xw[:].bitcast(I32), x_words[0].rearrange("p n r -> p (n r)").bitcast(I32))
        la_t = load_list("la_t", la)
        lb_t = load_list("lb_t", lb)
        gain = tile("gain", [P, PACK], F32)
        nc.sync.dma_start(gain[:], gn.rearrange("(p t) o -> p (t o)", t=PACK))
        w2_raw = tile("w2_raw", [P, PACK, N], F32)
        nc.sync.dma_start(w2_raw[:], w2.rearrange("(p j) c -> p j c", j=PACK))
        ma_t = load_list("ma_t", ma)
        mb_t = load_list("mb_t", mb)

        sums = [tile("sums%d" % t, [P, S], F32) for t in range(PACK)]
        for t in range(PACK):
            nc.vector.memset(sums[t][:], 0.0)

        sg = tile("sg", [P, S], U8)
        nc.vector.tensor_copy(sg[:], xs[:].indirect(offs_t[:]))

        order = (1, 2, 3, 0)
        lead = order[0]
        width = P * PACK
        w1_bf = {}
        for first, count, engine_copy in ((1, 1, nc.vector.tensor_copy), (2, 2, nc.scalar.copy), (0, 1, nc.scalar.copy)):
            grouped = tile("w1_bf%d" % first, [P, count, width], BF16)
            deal(engine_copy, grouped[:], w1_raw, first)
            for i in range(count):
                w1_bf[first + i] = grouped[:, i]
        lead_codes = tile("lead_codes", [P, P], U32)
        lead_scales = tile("lead_scales", [P, P], U8)
        quantize(lead_codes[:], lead_scales[:], w1_bf[lead])

        xg = tile("xg", [P, S], U32, "xs")
        y = [tile("y%d" % t, [P, S], F32) for t in range(PACK)]
        for u in range(2):
            cols = slice(u * HALF, (u + 1) * HALF)
            nc.vector.tensor_copy(xg[:, cols], xw[:].indirect(offs_t[:, u * 16 : (u + 1) * 16]))
        late_codes = tile("late_codes", [P, 3 * P], U32, "xw")
        late_scales = tile("late_scales", [P, 3 * P], U8)
        for i, t in enumerate(order[1:]):
            quantize(late_codes[:, i * P : (i + 1) * P], late_scales[:, i * P : (i + 1) * P], w1_bf[t])
        for i, (start, span) in enumerate(((0, HALF), (HALF, CHUNK), (HALF + CHUNK, CHUNK))):
            cols = slice(start, start + span)
            acc = bank(i, span)
            mx(acc[:], lead_codes[:], lead_scales[:], xg[:, cols], sg[:, cols])
            nc.scalar.copy(y[lead][:, cols], acc[:])
        for i, t in enumerate(order[1:]):
            cols = slice(i * P, (i + 1) * P)
            acc = bank(3 + i, S)
            mx(acc[:], late_codes[:, cols], late_scales[:, cols], xg[:], sg[:])
            nc.scalar.copy(y[t][:], acc[:])

        def fetch(dst, window, lst):
            nc.vector.tensor_copy(dst, window[:].indirect(lst[:]))

        a = [tile("a%d" % t, [P, V], F32) for t in range(PACK)]
        b = [tile("b%d" % t, [P, V], F32) for t in range(PACK)]
        z = [tile("z%d" % t, [P, 2 * S if t == 0 else S], F32) for t in range(PACK)]
        for t in order:
            fetch(a[t][:], y[t], la_t)
            fetch(b[t][:], y[t], lb_t)
        last = order[-1]

        def gained(dst, src, t):
            nc.scalar.activation(dst, src[t][:], COPY, scale=gain[:, t : t + 1])

        def place(t, lst, left, right, op):
            nc.vector.tensor_tensor(z[t][:].indirect(lst[:]), left, right, op)

        early = tile("early", [P, 3, V], F32, "y%d" % order[2])
        ga = {t: early[:, i] for i, t in enumerate(order[:-1])}
        for t in order[:-1]:
            gained(ga[t], a, t)
        for t in order[:-1]:
            place(t, lb_t, ga[t], b[t][:], MULT)

        w2_bf = tile("w2_bf", [P, PACK, width], BF16)
        for t in range(0, PACK, 2):
            deal(nc.scalar.copy, w2_bf[:, t : t + 2], w2_raw, t)

        middle = tile("middle", [P, 3, V], F32, "w2_raw")
        ga[last] = middle[:, 2]
        for i, t in enumerate(order[:2]):
            gained(middle[:, i], b, t)
        gained(ga[last], a, last)
        for i, t in enumerate(order[:2]):
            place(t, la_t, ga[t], middle[:, i], ADD)
        nc.scalar.copy(z[0][:, S:], z[1][:])
        place(last, lb_t, ga[last], b[last][:], MULT)
        late = tile("late", [P, 2, V], F32, "z1")
        for i, t in enumerate(order[2:]):
            gained(late[:, i], b, t)
        for i, t in enumerate(order[2:]):
            place(t, la_t, ga[t], late[:, i], ADD)

        w2_lead_codes = tile("w2_lead_codes", [P, P], U32, "b%d" % order[2])
        w2_lead_scales = tile("w2_lead_scales", [P, P], U8)
        quantize(w2_lead_codes[:], w2_lead_scales[:], w2_bf[:, 0])

        chunks = S // CHUNK
        zb = [tile("zb%d" % c, [P, CHUNK, PACK], BF16) for c in range(chunks)]
        for t in (2, 3):
            for c in range(chunks):
                nc.scalar.copy(zb[c][:, :, t], z[t][:, c * CHUNK : (c + 1) * CHUNK])
        low = z[0][:].rearrange("p (t n) -> p n t", t=2)
        for c in range(chunks):
            cast = nc.vector.tensor_copy if c < 2 else nc.scalar.copy
            cast(zb[c][:, :, 0:2], low[:, c * CHUNK : (c + 1) * CHUNK])

        z_codes = tile("z_codes", [P, S], U32)
        z_scales = tile("z_scales", [P, S], U8)
        h = [tile("h%d" % t, [P, S], F32) for t in range(PACK)]
        for c in range(chunks):
            cols = slice(c * CHUNK, (c + 1) * CHUNK)
            quantize(z_codes[:, cols], z_scales[:, cols], zb[c][:].rearrange("p n t -> p (n t)"))
            acc = bank((6 + c) % 8, CHUNK)
            mx(acc[:], w2_lead_codes[:], w2_lead_scales[:], z_codes[:, cols], z_scales[:, cols])
            nc.scalar.copy(h[0][:, cols], acc[:])
        w2_late_codes = tile("w2_late_codes", [P, 3 * P], U32, "zb2")
        w2_late_scales = tile("w2_late_scales", [P, 3 * P], U8)
        for t in range(1, PACK):
            cols = slice((t - 1) * P, t * P)
            quantize(w2_late_codes[:, cols], w2_late_scales[:, cols], w2_bf[:, t])
            acc = bank(1 + t, S)
            mx(acc[:], w2_late_codes[:, cols], w2_late_scales[:, cols], z_codes[:], z_scales[:])
            nc.scalar.copy(h[t][:], acc[:])

        cd = [tile("cd%d" % t, [P, 2 * V], F32) for t in range(PACK)]
        neg = [tile("neg%d" % t, [P, 2 * V], F32) for t in range(PACK)]
        res = [tile("res%d" % t, [P, S], F32) for t in range(PACK)]
        out_rows = out.rearrange("(p t) n -> t p n", t=PACK)
        for t in range(PACK):
            fetch(cd[t][:, :V], h[t], ma_t)
            fetch(cd[t][:, V:], h[t], mb_t)

        def finish(t):
            nc.scalar.activation(res[t][:], sums[t][:], ABS)
            nc.vector.tensor_tensor(res[t][:].indirect(mb_t[:]), cd[t][:, :V], neg[t][:, V:], ADD)
            nc.sync.dma_start(out_rows[t], res[t][:])

        for t in range(PACK):
            nc.scalar.activation(neg[t][:], cd[t][:], COPY, scale=-1.0)
            nc.vector.tensor_tensor(sums[t][:].indirect(ma_t[:]), neg[t][:, :V], neg[t][:, V:], ADD)
            if t > 0:
                finish(t - 1)
        finish(PACK - 1)
